import numpy as np
import ml_dtypes


def mxq(x, axis, fmt="e4m3"):
    dtype, down = {"e4m3": (ml_dtypes.float8_e4m3fn, 7), "e5m2": (ml_dtypes.float8_e5m2, 14)}[fmt]
    v = np.moveaxis(np.asarray(x, np.float32).astype(ml_dtypes.bfloat16).astype(np.float64), axis, -1)
    blocks = v.reshape(v.shape[:-1] + (-1, 32))
    amax = np.abs(blocks).max(-1, keepdims=True)
    byte = np.maximum(np.where(amax > 0, np.frexp(amax)[1] - 1 + 127, 0) - down, 1)
    scale = np.exp2(byte - 127.0)
    codes = (blocks / scale).astype(np.float32).astype(dtype).astype(np.float64)
    return np.moveaxis((codes * scale).reshape(v.shape), -1, axis)


WIDE = False


def mx_kscale(k):
    if not WIDE:
        return np.ones(k)
    levels = np.array([10, -10, 5, -5, 0])
    if k % 512:
        return np.exp2(np.random.permutation(np.resize(levels, k // 32))).repeat(32)
    a = np.empty((k // 512, 16))
    for p in range(k // 512):
        a[p, :8] = np.random.permutation(np.resize(levels, 8))
        for g in range(8):
            far = levels[np.abs(levels - a[p, g]) >= 10]
            a[p, g + 8] = far[np.random.randint(len(far))]
    return np.exp2(a.ravel()).repeat(32)


def f64(x):
    return np.asarray(x).astype(np.float64)


def striped(idx):
    return np.tile(idx.reshape(-1, 16).T, (8, 1)).astype(np.uint16)


def unstriped(offs):
    return offs[:16].T.reshape(-1).astype(np.int64)


E2M1 = np.array([0.0, 0.5, 1.0, 1.5, 2.0, 3.0, 4.0, 6.0, -0.0, -0.5, -1.0, -1.5, -2.0, -3.0, -4.0, -6.0])


def pack_weight(w, fmt):
    k, n = w.shape
    w = f64(np.asarray(w, np.float32).astype(ml_dtypes.bfloat16)).reshape(k // 32, 32, n)
    amax = np.abs(w).max(1)
    if fmt == "e4m3":
        byte = np.frexp(amax)[1] - 1 + 127 - 7
    else:
        mant, ex = np.frexp(amax / 6.0)
        byte = np.where(mant > 0.5, ex, ex - 1) + 127
    byte = np.clip(np.where(amax > 0, byte, 1), 1, 254)
    scaled = (w * np.exp2(127.0 - byte)[:, None, :]).reshape(k, n).astype(np.float32)
    by_word = np.ascontiguousarray(scaled.reshape(k // 512, 128, 4, n).transpose(0, 1, 3, 2))
    if fmt == "e4m3":
        words = by_word.astype(ml_dtypes.float8_e4m3fn).view(np.uint8)
    else:
        c = by_word.astype(ml_dtypes.float4_e2m1fn).view(np.uint8) & 0xF
        words = (c[..., 0::2] | (c[..., 1::2] << 4)).reshape(k // 512, 128, 2 * n)
    return np.ascontiguousarray(words), np.ascontiguousarray(byte.astype(np.uint8).reshape(k // 512, 16, n))


def unpack_weight(words, scales, fmt):
    g, _, n = scales.shape
    words = np.ascontiguousarray(words).reshape(g, 128, n, -1)
    if fmt == "e4m3":
        vals = words.view(ml_dtypes.float8_e4m3fn).astype(np.float64)
    else:
        nib = np.empty((g, 128, n, 4), np.uint8)
        nib[..., 0::2] = words & 0xF
        nib[..., 1::2] = words >> 4
        vals = E2M1[nib]
    vals = vals * np.repeat(np.exp2(scales.astype(np.float64) - 127.0), 8, axis=1)[..., None]
    return vals.transpose(0, 1, 3, 2).reshape(g * 512, n)


def gelu(v):
    return 0.5 * v * (1.0 + np.tanh(np.sqrt(2.0 / np.pi) * (v + 0.044715 * v**3)))


def striped8(idx):
    return np.concatenate([v.reshape(-1, 16).T for v in idx]).astype(np.uint16)


def unstriped8(offs):
    return np.stack([offs[16 * g:16 * g + 16].T.reshape(-1) for g in range(8)]).astype(np.int64)


def runs(v, idx8):
    k = np.arange(v.shape[0])
    return v[k[:, None], idx8[k % 512 // 64]]


K, T, S, H, P, N = 1024, 2048, 1024, 1024, 512, 512


def setup_inputs():
    n = np.random.standard_normal
    s = mx_kscale(K)[:, None]
    u = mx_kscale(H)[:, None]
    d = {}
    d["tab_words"], d["tab_scales"] = pack_weight(n((K, T)) * s, "e4m3")
    d["offs"] = striped8(np.stack([np.random.permutation(T)[:S] for _ in range(8)]))
    d["pos1"] = striped(np.random.permutation(S)[:P])
    d["pos2"] = striped(np.random.permutation(S)[:P])
    d["w1"] = (n((K, H)) / K ** 0.5 / s).astype(np.float32)
    d["bed"] = n((H, S)).astype(np.float32)
    d["gain"] = (np.exp(0.3 * n(H)) * u[:, 0]).astype(np.float32)
    d["w3"] = (n((H, N)) / H ** 0.5 / u).astype(np.float32)
    d["w4_words"], d["w4_scales"] = pack_weight(n((H, N)) / H ** 0.5 / u, "e2m1")
    return d


def reference(tab_words, tab_scales, offs, pos1, pos2, w1, bed, gain, w3, w4_words, w4_scales):
    v = runs(unpack_weight(tab_words, tab_scales, "e4m3"), unstriped8(offs))
    x = (mxq(f64(w1), 0, "e4m3").T @ v) + f64(bed)
    h = x / (1.0 + np.exp(-x))
    first = h[:, unstriped(pos1)]
    second = h[:, unstriped(pos2)]
    z = (first * second - first) * f64(gain)[:, None]
    zq = mxq(z, 0, "e4m3")
    y3 = mxq(f64(w3), 0, "e4m3").T @ zq
    y4 = unpack_weight(w4_words, w4_scales, "e2m1").T @ zq
    return np.minimum(y3, y4)

@@ -1,0 +1,278 @@
+from contextlib import ExitStack
+
+import concourse.mybir as mybir
+
+K, T, S, H, PAIRS, N = 1024, 2048, 1024, 1024, 512, 512
+FLOPS = 2 * K * H * S + 2 * 2 * H * N * PAIRS
+
+F32 = mybir.dt.float32
+BF16 = mybir.dt.bfloat16
+I32 = mybir.dt.int32
+U32 = mybir.dt.uint32
+U16 = mybir.dt.uint16
+U8 = mybir.dt.uint8
+FP8X4 = mybir.dt.float8_e4m3fn_x4
+FP4X4 = mybir.dt.float4_e2m1fn_x4
+ALU = mybir.AluOpType
+ACT = mybir.ActivationFunctionType
+
+P = 128
+PACK = 4
+PASS = P * PACK
+BANK = 512
+HALF = PAIRS // 2
+
+
+def tile_list_feeder_fault_scores_kernel(
+    tc, tab_words, tab_scales, offs, pos1, pos2, w1, bed, gain, w3, w4_words, w4_scales, out
+):
+    nc = tc.nc
+    with ExitStack() as ctx:
+        keep = ctx.enter_context(tc.tile_pool(name="keep", bufs=1))
+        raws = ctx.enter_context(tc.tile_pool(name="raws", bufs=3))
+        grps = ctx.enter_context(tc.tile_pool(name="grps", bufs=3))
+        hs = ctx.enter_context(tc.tile_pool(name="hs", bufs=5))
+        work = ctx.enter_context(tc.tile_pool(name="work", bufs=4))
+        psum = ctx.enter_context(tc.psum_pool(name="psum", bufs=8))
+
+        offs_sb = keep.tile([P, S // 16], U16, name="offs_sb")
+        pos1_sb = keep.tile([P, PAIRS // 16], U16, name="pos1_sb")
+        pos2_sb = keep.tile([P, PAIRS // 16], U16, name="pos2_sb")
+        gain_sb = keep.tile([P, 2, PACK], F32, name="gain_sb")
+        ngain = keep.tile([P, 2, PACK], F32, name="ngain")
+        warm = keep.tile([P, 1], F32, name="warm")
+        tabw = [keep.tile([P, T], U32, name=f"tabw{a}", align_bytes=64) for a in range(2)]
+        tabs = keep.tile([P, T], U8, name="tabs", align_bytes=64)
+        picked_s = keep.tile([P, S], U8, name="picked_s", align_bytes=64)
+        v_scales = keep.tile([P, S], U8, name="v_scales", align_bytes=64)
+        v_words = [keep.tile([P, S], U32, name=f"v_words{a}", align_bytes=64) for a in range(2)]
+        w1c = {(a, b): keep.tile([P, PASS], U32, name=f"w1c{a}{b}", align_bytes=64) for a in range(2) for b in range(2)}
+        w1s = {(a, b): keep.tile([P, PASS], U8, name=f"w1s{a}{b}", align_bytes=64) for a in range(2) for b in range(2)}
+        w3c = [keep.tile([P, N], U32, name=f"w3c{b}", align_bytes=64) for b in range(2)]
+        w3s = [keep.tile([P, N], U8, name=f"w3s{b}", align_bytes=64) for b in range(2)]
+        w4w = keep.tile([P, 2, 2 * N], U8, name="w4w", align_bytes=64)
+        w4s = keep.tile([P, 2, N], U8, name="w4s", align_bytes=64)
+        beds = [keep.tile([P, S], F32, name=f"bed{u}") for u in range(8)]
+        zf = [keep.tile([P, PACK, PAIRS], F32, name=f"zf{b}") for b in range(2)]
+        zb = {(b, c): keep.tile([P, HALF, PACK], BF16, name=f"zb{b}{c}", align_bytes=64) for b in range(2) for c in range(2)}
+        zc = {(b, c): keep.tile([P, HALF], U32, name=f"zc{b}{c}", align_bytes=64) for b in range(2) for c in range(2)}
+        zs = {(b, c): keep.tile([P, HALF], U8, name=f"zs{b}{c}", align_bytes=64) for b in range(2) for c in range(2)}
+
+        bed_rows = bed.rearrange("(b p t) j -> b t p j", b=2, t=PACK)
+
+        def load_tab(a):
+            nc.sync.dma_start(tabw[a][:].bitcast(I32), tab_words[a].rearrange("p t i -> p (t i)").bitcast(I32))
+
+        def load_raw(w, a, c0, width):
+            raw = raws.tile([P, PACK, width], F32, name="raw")
+            nc.sync.dma_start(raw[:], w[a * PASS : (a + 1) * PASS, c0 : c0 + width].rearrange("(p i) c -> p i c", i=PACK))
+            return raw
+
+        def load_bed(u):
+            nc.sync.dma_start(beds[u][:], bed_rows[u // PACK, u % PACK])
+
+        def cast_w1(grouped, raw, r0, q0, nq):
+            nc.scalar.copy(
+                grouped[:].rearrange("p (t q i) -> p q t i", t=PACK, i=PACK)[:, q0 : q0 + nq],
+                raw[:].rearrange("p i (q t) -> p q t i", t=PACK)[:, r0 : r0 + nq],
+            )
+
+        def cast_w3(grouped, raw, c0, width):
+            nc.scalar.copy(
+                grouped[:].rearrange("p (c i) -> p c i", i=PACK)[:, c0 : c0 + width],
+                raw[:].rearrange("p i c -> p c i")[:, c0 : c0 + width],
+            )
+
+        def new_group():
+            return grps.tile([P, PASS * PACK], BF16, name="grouped", align_bytes=64)
+
+        def quantize(codes, scales, src):
+            nc.vector.quantize_mx(out=codes.bitcast(FP8X4), scales=scales, in_=src)
+
+        nc.vector.memset(tabs[:].bitcast(I32), 0)
+        nc.gpsimd.memset(w4s[:].rearrange("p b c -> p (b c)").bitcast(I32), 0)
+        nc.gpsimd.memset(warm[:], 0.0)
+        nc.scalar.activation(warm[:], warm[:], ACT.Silu)
+        nc.sync.dma_start(offs_sb[:], offs)
+        load_tab(0)
+        for a in range(2):
+            rows = tab_scales[a].rearrange("(g e) t -> e g t", e=2)
+            for e in range(2):
+                nc.sync.dma_start(tabs[4 * a + e : P : 16, :].bitcast(I32), rows[e].bitcast(I32))
+        raw00 = load_raw(w1, 0, 0, PASS)
+        load_tab(1)
+        raw10 = [load_raw(w1, 1, c * 256, 256) for c in range(2)]
+        nc.sync.dma_start(pos2_sb[:], pos2)
+        nc.sync.dma_start(pos1_sb[:], pos1)
+        nc.sync.dma_start(gain_sb[:], gain.rearrange("(b p t) -> p b t", b=2, t=PACK))
+        nc.sync.dma_start(w4w[:].bitcast(I32), w4_words.rearrange("b p c -> p b c").bitcast(I32))
+
+        nc.vector.tensor_copy(v_words[0][:], tabw[0][:].indirect(offs_sb[:]))
+        nc.vector.tensor_copy(picked_s[:], tabs[:].indirect(offs_sb[:]))
+        nc.vector.tensor_copy(v_scales[:].bitcast(I32), picked_s[:].bitcast(I32))
+        g00 = new_group()
+        cast_w1(g00, raw00, 0, 0, P)
+        for a in range(2):
+            for e in range(2):
+                nc.sync.dma_start(
+                    v_scales[4 * a + 2 + e : P : 32, :].bitcast(I32),
+                    picked_s[16 + 4 * a + e : P : 32, :].bitcast(I32),
+                )
+        for c in range(2):
+            nc.vector.tensor_copy(
+                v_words[1][:, c * BANK : (c + 1) * BANK], tabw[1][:].indirect(offs_sb[:, c * 32 : (c + 1) * 32])
+            )
+        quantize(w1c[0, 0][:], w1s[0, 0][:], g00[:])
+        g10 = new_group()
+        for c in range(2):
+            cast_w1(g10, raw10[c], 0, c * 64, 64)
+        for c in range(2):
+            quantize(w1c[1, 0][:, c * 256 : (c + 1) * 256], w1s[1, 0][:, c * 256 : (c + 1) * 256], g10[:, c * 1024 : (c + 1) * 1024])
+        nc.gpsimd.tensor_scalar(ngain[:], gain_sb[:], -1.0, 0.0, ALU.mult, ALU.add)
+
+        for u in (0, 1, 2):
+            load_bed(u)
+        raw_next = [load_raw(w1, 0, PASS, PASS)]
+        load_bed(3)
+        raw_next.append(load_raw(w1, 1, PASS, PASS))
+        for u in range(4, 8):
+            load_bed(u)
+        raw_next.extend(load_raw(w3, b, 0, N) for b in range(2))
+        for d in range(4):
+            nc.sync.dma_start(
+                w4s[32 * d : 32 * d + 4].bitcast(I32),
+                w4_scales[:, 4 * d : 4 * d + 4, :].rearrange("b q c -> q b c").bitcast(I32),
+            )
+
+        h = {}
+        factor = {}
+
+        def first_stage(u):
+            b, t = divmod(u, PACK)
+            cols = slice(t * P, (t + 1) * P)
+            for c in range(2):
+                js = slice(c * BANK, (c + 1) * BANK)
+                acc = psum.tile([P, BANK], F32, name="acc")
+                for a in range(2):
+                    nc.tensor.matmul_mx(
+                        out=acc[:],
+                        lhsT=w1c[a, b][:, cols].bitcast(FP8X4),
+                        lhsT_scale=w1s[a, b][:, cols],
+                        rhs=v_words[a][:, js].bitcast(FP8X4),
+                        rhs_scale=v_scales[4 * a : P, js],
+                        start=(a == 0),
+                        stop=(a == 1),
+                    )
+                nc.vector.tensor_tensor(beds[u][:, js], acc[:], beds[u][:, js], ALU.add)
+            h[u] = hs.tile([P, S], F32, name="h")
+            nc.scalar.activation(h[u][:], beds[u][:], ACT.Silu)
+
+        def second_course(u):
+            b, t = divmod(u, PACK)
+            second = work.tile([P, PAIRS], F32, name="second")
+            nc.vector.tensor_copy(second[:], h[u][:].indirect(pos2_sb[:]))
+            factor[u] = work.tile([P, PAIRS], F32, name="factor")
+            nc.scalar.activation(
+                factor[u][:], second[:], ACT.Identity, bias=ngain[:, b, t : t + 1], scale=gain_sb[:, b, t : t + 1]
+            )
+
+        def first_course(u, m0, width):
+            b, t = divmod(u, PACK)
+            nc.vector.tensor_tensor(
+                zf[b][:, t, m0 : m0 + width],
+                h[u][:].indirect(pos1_sb[:, m0 // 16 : (m0 + width) // 16]),
+                factor[u][:, m0 : m0 + width],
+                ALU.mult,
+            )
+
+        def round_z(b, c):
+            nc.scalar.copy(zb[b, c][:], zf[b][:, :, c * HALF : (c + 1) * HALF].rearrange("p t m -> p m t"))
+
+        def quantize_z(b, c):
+            quantize(zc[b, c][:], zs[b, c][:], zb[b, c][:].rearrange("p m t -> p (m t)"))
+
+        scores = {}
+
+        def second_stage(b, c):
+            for n in range(4):
+                if b == 0:
+                    scores[n, c] = psum.tile([P, BANK], F32, name="acc")
+                acc = scores[n, c]
+                cols = slice(n * P, (n + 1) * P)
+                nc.tensor.matmul_mx(
+                    out=acc[:, 0:HALF],
+                    lhsT=w3c[b][:, cols].bitcast(FP8X4),
+                    lhsT_scale=w3s[b][:, cols],
+                    rhs=zc[b, c][:].bitcast(FP8X4),
+                    rhs_scale=zs[b, c][:],
+                    start=(b == 0),
+                    stop=False,
+                )
+                for s in range(2):
+                    ms = slice(s * P, (s + 1) * P)
+                    nc.tensor.matmul_mx(
+                        out=acc[:, HALF + s * P : HALF + (s + 1) * P],
+                        lhsT=w4w[:, b, 2 * n * P : 2 * (n + 1) * P].bitcast(FP4X4),
+                        lhsT_scale=w4s[:, b, cols],
+                        rhs=zc[b, c][:, ms].bitcast(FP8X4),
+                        rhs_scale=zs[b, c][:, ms],
+                        start=False,
+                        stop=(b == 1 and s == 1),
+                    )
+
+        def finish(c):
+            for n in range(4):
+                y3 = work.tile([P, HALF], F32, name="y3")
+                nc.scalar.copy(y3[:], scores[n, c][:, 0:HALF])
+                res = work.tile([P, HALF], F32, name="res")
+                nc.vector.tensor_tensor(res[:], scores[n, c][:, HALF : 2 * HALF], y3[:], ALU.min)
+                nc.sync.dma_start(out[n * P : (n + 1) * P, c * HALF : (c + 1) * HALF], res[:])
+
+        groups = {}
+
+        def later_weight(piece):
+            idx, c = divmod(piece, 2)
+            if c == 0:
+                groups[idx] = new_group()
+            if idx < 2:
+                cast_w1(groups[idx], raw_next[idx], c * 64, c * 64, 64)
+                codes, scales = w1c[idx, 1], w1s[idx, 1]
+            else:
+                cast_w3(groups[idx], raw_next[idx], c * 256, 256)
+                codes, scales = w3c[idx - 2], w3s[idx - 2]
+            if c == 1:
+                quantize(codes[:], scales[:], groups[idx][:])
+
+        first_stage(0)
+        for u in range(8):
+            if u + 1 < 8:
+                first_stage(u + 1)
+            second_course(u)
+            if u < 2:
+                later_weight(2 * u)
+                later_weight(2 * u + 1)
+            elif u < 6:
+                later_weight(u + 2)
+            if 1 <= u <= 4:
+                first_course(u - 1, 0, PAIRS)
+            elif u > 4:
+                first_course(u - 1, 0, HALF)
+            if u in (4, 5):
+                round_z(0, u - 4)
+            if u in (5, 6):
+                quantize_z(0, u - 5)
+        first_course(7, 0, HALF)
+        second_stage(0, 0)
+        second_stage(0, 1)
+        round_z(1, 0)
+        first_course(4, HALF, HALF)
+        first_course(5, HALF, HALF)
+        quantize_z(1, 0)
+        second_stage(1, 0)
+        first_course(6, HALF, HALF)
+        first_course(7, HALF, HALF)
+        round_z(1, 1)
+        finish(0)
+        quantize_z(1, 1)
+        second_stage(1, 1)
+        finish(1)

@@ -29,10 +29,11 @@ def tile_list_feeder_fault_scores_kernel(
     nc = tc.nc
     with ExitStack() as ctx:
         keep = ctx.enter_context(tc.tile_pool(name="keep", bufs=1))
-        raws = ctx.enter_context(tc.tile_pool(name="raws", bufs=3))
+        raws = ctx.enter_context(tc.tile_pool(name="raws", bufs=4))
         grps = ctx.enter_context(tc.tile_pool(name="grps", bufs=3))
         hs = ctx.enter_context(tc.tile_pool(name="hs", bufs=5))
         work = ctx.enter_context(tc.tile_pool(name="work", bufs=4))
+        seconds = ctx.enter_context(tc.tile_pool(name="seconds", bufs=2))
         psum = ctx.enter_context(tc.psum_pool(name="psum", bufs=8))
 
         offs_sb = keep.tile([P, S // 16], U16, name="offs_sb")
@@ -53,9 +54,13 @@ def tile_list_feeder_fault_scores_kernel(
         w4w = keep.tile([P, 2, 2 * N], U8, name="w4w", align_bytes=64)
         w4s = keep.tile([P, 2, N], U8, name="w4s", align_bytes=64)
         beds = [keep.tile([P, S], F32, name=f"bed{u}") for u in range(8)]
-        zf = [keep.tile([P, PACK, PAIRS], F32, name=f"zf{b}") for b in range(2)]
-        zb = {(b, c): keep.tile([P, HALF, PACK], BF16, name=f"zb{b}{c}", align_bytes=64) for b in range(2) for c in range(2)}
-        zc = {(b, c): keep.tile([P, HALF], U32, name=f"zc{b}{c}", align_bytes=64) for b in range(2) for c in range(2)}
+        zf = {0: keep.tile([P, PACK, PAIRS], F32, name="zf0"), (1, 0): keep.tile([P, PACK, HALF], F32, name="zf10"), }
+        last = keep.tile([P, PACK * HALF], F32, name="last", align_bytes=64)
+        zb = {(b, c): keep.tile([P, HALF, PACK], BF16, name=f"zb{b}{c}", align_bytes=64) for b, c in ((0, 0), (0, 1), (1, 1))}
+        zb = {key: tile[:].rearrange("p m t -> p (m t)") for key, tile in zb.items()}
+        zb[1, 0] = last[:, PAIRS : 2 * PAIRS].bitcast(BF16)
+        zf = {0: zf[0][:], (1, 0): zf[1, 0][:], (1, 1): last[:].rearrange("p (t m) -> p t m", t=PACK)}
+        zc = {(b, c): keep.tile([P, HALF], U32, name=f"zc{b}{c}", align_bytes=64) for b, c in ((0, 0), (1, 0), (1, 1))}
         zs = {(b, c): keep.tile([P, HALF], U8, name=f"zs{b}{c}", align_bytes=64) for b in range(2) for c in range(2)}
 
         bed_rows = bed.rearrange("(b p t) j -> b t p j", b=2, t=PACK)
@@ -64,7 +69,7 @@ def tile_list_feeder_fault_scores_kernel(
             nc.sync.dma_start(tabw[a][:].bitcast(I32), tab_words[a].rearrange("p t i -> p (t i)").bitcast(I32))
 
         def load_raw(w, a, c0, width):
-            raw = raws.tile([P, PACK, width], F32, name="raw")
+            raw = raws.tile([P, PACK, width], F32, name=f"raw{width}")
             nc.sync.dma_start(raw[:], w[a * PASS : (a + 1) * PASS, c0 : c0 + width].rearrange("(p i) c -> p i c", i=PACK))
             return raw
 
@@ -73,14 +78,14 @@ def tile_list_feeder_fault_scores_kernel(
 
         def cast_w1(grouped, raw, r0, q0, nq):
             nc.scalar.copy(
-                grouped[:].rearrange("p (t q i) -> p q t i", t=PACK, i=PACK)[:, q0 : q0 + nq],
-                raw[:].rearrange("p i (q t) -> p q t i", t=PACK)[:, r0 : r0 + nq],
+                grouped[:].rearrange("p (t q i) -> p q i t", t=PACK, i=PACK)[:, q0 : q0 + nq],
+                raw[:].rearrange("p i (q t) -> p q i t", t=PACK)[:, r0 : r0 + nq],
             )
 
         def cast_w3(grouped, raw, c0, width):
             nc.scalar.copy(
-                grouped[:].rearrange("p (c i) -> p c i", i=PACK)[:, c0 : c0 + width],
-                raw[:].rearrange("p i c -> p c i")[:, c0 : c0 + width],
+                grouped[:].rearrange("p (c n i) -> p c i n", n=PACK, i=PACK)[:, c0 // PACK : (c0 + width) // PACK],
+                raw[:].rearrange("p i (c n) -> p c i n", n=PACK)[:, c0 // PACK : (c0 + width) // PACK],
             )
 
         def new_group():
@@ -94,50 +99,52 @@ def tile_list_feeder_fault_scores_kernel(
         nc.gpsimd.memset(warm[:], 0.0)
         nc.scalar.activation(warm[:], warm[:], ACT.Silu)
         nc.sync.dma_start(offs_sb[:], offs)
-        load_tab(0)
+        raw00 = [load_raw(w1, 0, c * 256, 256) for c in range(2)]
         for a in range(2):
             rows = tab_scales[a].rearrange("(g e) t -> e g t", e=2)
             for e in range(2):
-                nc.sync.dma_start(tabs[4 * a + e : P : 16, :].bitcast(I32), rows[e].bitcast(I32))
-        raw00 = load_raw(w1, 0, 0, PASS)
-        load_tab(1)
+                nc.sync.dma_start(tabs[8 * a + e : P : 16, :].bitcast(I32), rows[e].bitcast(I32))
+        load_tab(0)
         raw10 = [load_raw(w1, 1, c * 256, 256) for c in range(2)]
+        load_tab(1)
+        load_bed(0)
         nc.sync.dma_start(pos2_sb[:], pos2)
         nc.sync.dma_start(pos1_sb[:], pos1)
         nc.sync.dma_start(gain_sb[:], gain.rearrange("(b p t) -> p b t", b=2, t=PACK))
-        nc.sync.dma_start(w4w[:].bitcast(I32), w4_words.rearrange("b p c -> p b c").bitcast(I32))
 
-        nc.vector.tensor_copy(v_words[0][:], tabw[0][:].indirect(offs_sb[:]))
         nc.vector.tensor_copy(picked_s[:], tabs[:].indirect(offs_sb[:]))
         nc.vector.tensor_copy(v_scales[:].bitcast(I32), picked_s[:].bitcast(I32))
+        nc.vector.tensor_copy(v_words[0][:], tabw[0][:].indirect(offs_sb[:]))
         g00 = new_group()
-        cast_w1(g00, raw00, 0, 0, P)
-        for a in range(2):
-            for e in range(2):
-                nc.sync.dma_start(
-                    v_scales[4 * a + 2 + e : P : 32, :].bitcast(I32),
-                    picked_s[16 + 4 * a + e : P : 32, :].bitcast(I32),
-                )
         for c in range(2):
-            nc.vector.tensor_copy(
-                v_words[1][:, c * BANK : (c + 1) * BANK], tabw[1][:].indirect(offs_sb[:, c * 32 : (c + 1) * 32])
+            cast_w1(g00, raw00[c], 0, c * 64, 64)
+        for e in range(2):
+            nc.sync.dma_start(
+                v_scales[2 + e : P - 16 : 8, :].bitcast(I32),
+                picked_s[16 + e : P : 8, :].bitcast(I32),
             )
         quantize(w1c[0, 0][:], w1s[0, 0][:], g00[:])
         g10 = new_group()
         for c in range(2):
             cast_w1(g10, raw10[c], 0, c * 64, 64)
+        quantize(w1c[1, 0][:], w1s[1, 0][:], g10[:])
         for c in range(2):
-            quantize(w1c[1, 0][:, c * 256 : (c + 1) * 256], w1s[1, 0][:, c * 256 : (c + 1) * 256], g10[:, c * 1024 : (c + 1) * 1024])
+            nc.vector.tensor_copy(
+                v_words[1][:, c * BANK : (c + 1) * BANK], tabw[1][:].indirect(offs_sb[:, c * 32 : (c + 1) * 32])
+            )
         nc.gpsimd.tensor_scalar(ngain[:], gain_sb[:], -1.0, 0.0, ALU.mult, ALU.add)
 
-        for u in (0, 1, 2):
-            load_bed(u)
         raw_next = [load_raw(w1, 0, PASS, PASS)]
-        load_bed(3)
-        raw_next.append(load_raw(w1, 1, PASS, PASS))
-        for u in range(4, 8):
+        for u in (1, 2):
             load_bed(u)
-        raw_next.extend(load_raw(w3, b, 0, N) for b in range(2))
+        raw_next.append(load_raw(w1, 1, PASS, PASS))
+        load_bed(3)
+        for b in range(2):
+            raw_next.append(load_raw(w3, b, 0, N))
+            load_bed(4 + b)
+        for u in (6, 7):
+            load_bed(u)
+        nc.sync.dma_start(w4w[:].bitcast(I32), w4_words.rearrange("b p c -> p b c").bitcast(I32))
         for d in range(4):
             nc.sync.dma_start(
                 w4s[32 * d : 32 * d + 4].bitcast(I32),
@@ -159,7 +166,7 @@ def tile_list_feeder_fault_scores_kernel(
                         lhsT=w1c[a, b][:, cols].bitcast(FP8X4),
                         lhsT_scale=w1s[a, b][:, cols],
                         rhs=v_words[a][:, js].bitcast(FP8X4),
-                        rhs_scale=v_scales[4 * a : P, js],
+                        rhs_scale=v_scales[8 * a : P, js],
                         start=(a == 0),
                         stop=(a == 1),
                     )
@@ -169,64 +176,79 @@ def tile_list_feeder_fault_scores_kernel(
 
         def second_course(u):
             b, t = divmod(u, PACK)
-            second = work.tile([P, PAIRS], F32, name="second")
-            nc.vector.tensor_copy(second[:], h[u][:].indirect(pos2_sb[:]))
-            factor[u] = work.tile([P, PAIRS], F32, name="factor")
+            if u == 7:
+                second = last[:, 0:PAIRS]
+            else:
+                second = seconds.tile([P, PAIRS], F32, name="second")[:]
+            nc.vector.tensor_copy(second, h[u][:].indirect(pos2_sb[:]))
+            factor[u] = work.tile([P, PAIRS], F32, name="factor", align_bytes=64)
             nc.scalar.activation(
-                factor[u][:], second[:], ACT.Identity, bias=ngain[:, b, t : t + 1], scale=gain_sb[:, b, t : t + 1]
+                factor[u][:], second, ACT.Identity, bias=ngain[:, b, t : t + 1], scale=gain_sb[:, b, t : t + 1]
             )
 
         def first_course(u, m0, width):
             b, t = divmod(u, PACK)
             nc.vector.tensor_tensor(
-                zf[b][:, t, m0 : m0 + width],
+                zf[0][:, t, :] if b == 0 else zf[1, m0 // HALF][:, t, :],
                 h[u][:].indirect(pos1_sb[:, m0 // 16 : (m0 + width) // 16]),
                 factor[u][:, m0 : m0 + width],
                 ALU.mult,
             )
 
-        def round_z(b, c):
-            nc.scalar.copy(zb[b, c][:], zf[b][:, :, c * HALF : (c + 1) * HALF].rearrange("p t m -> p m t"))
+        def round_z(b, c, copy):
+            src = zf[0][:, :, c * HALF : (c + 1) * HALF] if b == 0 else zf[1, c]
+            copy(
+                zb[b, c].rearrange("p (m n t) -> p m t n", n=PACK, t=PACK),
+                src.rearrange("p t (m n) -> p m t n", n=PACK),
+            )
 
         def quantize_z(b, c):
-            quantize(zc[b, c][:], zs[b, c][:], zb[b, c][:].rearrange("p m t -> p (m t)"))
+            quantize(zc[b, c][:], zs[b, c][:], zb[b, c])
 
         scores = {}
 
         def second_stage(b, c):
-            for n in range(4):
+            for pair in range(2):
                 if b == 0:
-                    scores[n, c] = psum.tile([P, BANK], F32, name="acc")
-                acc = scores[n, c]
-                cols = slice(n * P, (n + 1) * P)
-                nc.tensor.matmul_mx(
-                    out=acc[:, 0:HALF],
-                    lhsT=w3c[b][:, cols].bitcast(FP8X4),
-                    lhsT_scale=w3s[b][:, cols],
-                    rhs=zc[b, c][:].bitcast(FP8X4),
-                    rhs_scale=zs[b, c][:],
-                    start=(b == 0),
-                    stop=False,
-                )
-                for s in range(2):
-                    ms = slice(s * P, (s + 1) * P)
+                    scores[3, pair, c] = psum.tile([P, BANK], F32, name="acc")
+                    scores[4, pair, c] = psum.tile([P, BANK], F32, name="acc")
+                for k in range(2):
+                    n = 2 * pair + k
+                    cols = slice(n * P, (n + 1) * P)
                     nc.tensor.matmul_mx(
-                        out=acc[:, HALF + s * P : HALF + (s + 1) * P],
-                        lhsT=w4w[:, b, 2 * n * P : 2 * (n + 1) * P].bitcast(FP4X4),
-                        lhsT_scale=w4s[:, b, cols],
-                        rhs=zc[b, c][:, ms].bitcast(FP8X4),
-                        rhs_scale=zs[b, c][:, ms],
-                        start=False,
-                        stop=(b == 1 and s == 1),
+                        out=scores[3, pair, c][:, k * HALF : (k + 1) * HALF],
+                        lhsT=w3c[b][:, cols].bitcast(FP8X4),
+                        lhsT_scale=w3s[b][:, cols],
+                        rhs=zc[b, c][:].bitcast(FP8X4),
+                        rhs_scale=zs[b, c][:],
+                        start=(b == 0 and k == 0),
+                        stop=(b == 1 and k == 1),
                     )
+                for k in range(2):
+                    n = 2 * pair + k
+                    cols = slice(n * P, (n + 1) * P)
+                    for s in range(2):
+                        ms = slice(s * P, (s + 1) * P)
+                        nc.tensor.matmul_mx(
+                            out=scores[4, pair, c][:, k * HALF + s * P : k * HALF + (s + 1) * P],
+                            lhsT=w4w[:, b, 2 * n * P : 2 * (n + 1) * P].bitcast(FP4X4),
+                            lhsT_scale=w4s[:, b, cols],
+                            rhs=zc[b, c][:, ms].bitcast(FP8X4),
+                            rhs_scale=zs[b, c][:, ms],
+                            start=(b == 0 and k == 0 and s == 0),
+                            stop=(b == 1 and k == 1 and s == 1),
+                        )
 
         def finish(c):
-            for n in range(4):
-                y3 = work.tile([P, HALF], F32, name="y3")
-                nc.scalar.copy(y3[:], scores[n, c][:, 0:HALF])
-                res = work.tile([P, HALF], F32, name="res")
-                nc.vector.tensor_tensor(res[:], scores[n, c][:, HALF : 2 * HALF], y3[:], ALU.min)
-                nc.sync.dma_start(out[n * P : (n + 1) * P, c * HALF : (c + 1) * HALF], res[:])
+            for pair in range(2):
+                y3 = work.tile([P, BANK], F32, name="y3")
+                nc.scalar.copy(y3[:], scores[3, pair, c][:])
+                res = work.tile([P, BANK], F32, name="res")
+                nc.vector.tensor_tensor(res[:], scores[4, pair, c][:], y3[:], ALU.min)
+                nc.sync.dma_start(
+                    out[2 * pair * P : 2 * (pair + 1) * P, c * HALF : (c + 1) * HALF].rearrange("(k p) m -> p k m", k=2),
+                    res[:].rearrange("p (k m) -> p k m", k=2),
+                )
 
         groups = {}
 
@@ -248,31 +270,31 @@ def tile_list_feeder_fault_scores_kernel(
             if u + 1 < 8:
                 first_stage(u + 1)
             second_course(u)
-            if u < 2:
+            if u < 4:
                 later_weight(2 * u)
                 later_weight(2 * u + 1)
-            elif u < 6:
-                later_weight(u + 2)
             if 1 <= u <= 4:
                 first_course(u - 1, 0, PAIRS)
             elif u > 4:
                 first_course(u - 1, 0, HALF)
             if u in (4, 5):
-                round_z(0, u - 4)
-            if u in (5, 6):
-                quantize_z(0, u - 5)
+                round_z(0, u - 4, nc.scalar.copy)
+            if u == 5:
+                quantize_z(0, 0)
         first_course(7, 0, HALF)
         second_stage(0, 0)
-        second_stage(0, 1)
-        round_z(1, 0)
+        round_z(1, 0, nc.scalar.copy)
         first_course(4, HALF, HALF)
         first_course(5, HALF, HALF)
         quantize_z(1, 0)
         second_stage(1, 0)
+        zc[0, 1] = work.tile([P, HALF], U32, name="factor", align_bytes=64)
+        quantize_z(0, 1)
+        second_stage(0, 1)
         first_course(6, HALF, HALF)
         first_course(7, HALF, HALF)
-        round_z(1, 1)
-        finish(0)
+        round_z(1, 1, nc.vector.tensor_copy)
         quantize_z(1, 1)
         second_stage(1, 1)
+        finish(0)
         finish(1)

@@ -17,10 +17,16 @@ ALU = mybir.AluOpType
 ACT = mybir.ActivationFunctionType
 
 P = 128
+GROUP = 16
 PACK = 4
 PASS = P * PACK
+PASSES = 2
+SLICES = PASSES * PACK
 BANK = 512
 HALF = PAIRS // 2
+PIECE = PASS // 2
+PLANE_STEP = 8
+BOTH = range(2)
 
 
 def tile_list_feeder_fault_scores_kernel(
@@ -30,270 +36,259 @@ def tile_list_feeder_fault_scores_kernel(
     with ExitStack() as ctx:
         keep = ctx.enter_context(tc.tile_pool(name="keep", bufs=1))
         raws = ctx.enter_context(tc.tile_pool(name="raws", bufs=4))
-        grps = ctx.enter_context(tc.tile_pool(name="grps", bufs=3))
-        hs = ctx.enter_context(tc.tile_pool(name="hs", bufs=5))
-        work = ctx.enter_context(tc.tile_pool(name="work", bufs=4))
+        rounded = ctx.enter_context(tc.tile_pool(name="rounded", bufs=3))
+        hs = ctx.enter_context(tc.tile_pool(name="hs", bufs=PACK + 1))
+        work = ctx.enter_context(tc.tile_pool(name="work", bufs=PACK))
         seconds = ctx.enter_context(tc.tile_pool(name="seconds", bufs=2))
         psum = ctx.enter_context(tc.psum_pool(name="psum", bufs=8))
 
-        offs_sb = keep.tile([P, S // 16], U16, name="offs_sb")
-        pos1_sb = keep.tile([P, PAIRS // 16], U16, name="pos1_sb")
-        pos2_sb = keep.tile([P, PAIRS // 16], U16, name="pos2_sb")
-        gain_sb = keep.tile([P, 2, PACK], F32, name="gain_sb")
-        ngain = keep.tile([P, 2, PACK], F32, name="ngain")
-        warm = keep.tile([P, 1], F32, name="warm")
-        tabw = [keep.tile([P, T], U32, name=f"tabw{a}", align_bytes=64) for a in range(2)]
-        tabs = keep.tile([P, T], U8, name="tabs", align_bytes=64)
-        picked_s = keep.tile([P, S], U8, name="picked_s", align_bytes=64)
+        def mx_tiles(name, dtype, width, keys):
+            return {key: keep.tile([P, width], dtype, name=f"{name}{n}", align_bytes=64) for n, key in enumerate(keys)}
+
+        pass_pairs = [(a, b) for a in BOTH for b in BOTH]
+        offs_sb = keep.tile([P, S // GROUP], U16, name="offs_sb")
+        pos1_sb = keep.tile([P, PAIRS // GROUP], U16, name="pos1_sb")
+        pos2_sb = keep.tile([P, PAIRS // GROUP], U16, name="pos2_sb")
+        gain_sb = keep.tile([P, PASSES, PACK], F32, name="gain_sb")
+        minus_gain = keep.tile([P, PASSES, PACK], F32, name="minus_gain")
+        table_words = mx_tiles("table_words", U32, T, BOTH)
+        table_scales = keep.tile([P, T], U8, name="table_scales", align_bytes=64)
+        picked_scales = keep.tile([P, S], U8, name="picked_scales", align_bytes=64)
         v_scales = keep.tile([P, S], U8, name="v_scales", align_bytes=64)
-        v_words = [keep.tile([P, S], U32, name=f"v_words{a}", align_bytes=64) for a in range(2)]
-        w1c = {(a, b): keep.tile([P, PASS], U32, name=f"w1c{a}{b}", align_bytes=64) for a in range(2) for b in range(2)}
-        w1s = {(a, b): keep.tile([P, PASS], U8, name=f"w1s{a}{b}", align_bytes=64) for a in range(2) for b in range(2)}
-        w3c = [keep.tile([P, N], U32, name=f"w3c{b}", align_bytes=64) for b in range(2)]
-        w3s = [keep.tile([P, N], U8, name=f"w3s{b}", align_bytes=64) for b in range(2)]
-        w4w = keep.tile([P, 2, 2 * N], U8, name="w4w", align_bytes=64)
-        w4s = keep.tile([P, 2, N], U8, name="w4s", align_bytes=64)
-        beds = [keep.tile([P, S], F32, name=f"bed{u}") for u in range(8)]
-        zf = {0: keep.tile([P, PACK, PAIRS], F32, name="zf0"), (1, 0): keep.tile([P, PACK, HALF], F32, name="zf10"), }
-        last = keep.tile([P, PACK * HALF], F32, name="last", align_bytes=64)
-        zb = {(b, c): keep.tile([P, HALF, PACK], BF16, name=f"zb{b}{c}", align_bytes=64) for b, c in ((0, 0), (0, 1), (1, 1))}
-        zb = {key: tile[:].rearrange("p m t -> p (m t)") for key, tile in zb.items()}
-        zb[1, 0] = last[:, PAIRS : 2 * PAIRS].bitcast(BF16)
-        zf = {0: zf[0][:], (1, 0): zf[1, 0][:], (1, 1): last[:].rearrange("p (t m) -> p t m", t=PACK)}
-        zc = {(b, c): keep.tile([P, HALF], U32, name=f"zc{b}{c}", align_bytes=64) for b, c in ((0, 0), (1, 0), (1, 1))}
-        zs = {(b, c): keep.tile([P, HALF], U8, name=f"zs{b}{c}", align_bytes=64) for b in range(2) for c in range(2)}
+        v_words = mx_tiles("v_words", U32, S, BOTH)
+        w1_codes = mx_tiles("w1_codes", U32, PASS, pass_pairs)
+        w1_scales = mx_tiles("w1_scales", U8, PASS, pass_pairs)
+        w3_codes = mx_tiles("w3_codes", U32, N, BOTH)
+        w3_scales = mx_tiles("w3_scales", U8, N, BOTH)
+        w4_sb = keep.tile([P, PASSES, 2 * N], U8, name="w4_sb", align_bytes=64)
+        w4_scales_sb = keep.tile([P, PASSES, N], U8, name="w4_scales_sb", align_bytes=64)
+        x = [keep.tile([P, S], F32, name=f"x{u}") for u in range(SLICES)]
 
-        bed_rows = bed.rearrange("(b p t) j -> b t p j", b=2, t=PACK)
+        z_first = keep.tile([P, PACK, PAIRS], F32, name="z_first")
+        z_last_low = keep.tile([P, PACK, HALF], F32, name="z_last_low")
+        tail = keep.tile([P, PACK * HALF], F32, name="tail", align_bytes=64)
+        z_f32 = {(0, c): z_first[:, :, c * HALF : (c + 1) * HALF] for c in BOTH}
+        z_f32[1, 0] = z_last_low[:]
+        z_f32[1, 1] = tail[:].rearrange("p (t m) -> p t m", t=PACK)
+        z_bf16 = {key: tile[:] for key, tile in mx_tiles("z_bf16", BF16, PACK * HALF, [(0, 0), (0, 1), (1, 1)]).items()}
+        z_bf16[1, 0] = tail[:, PAIRS : 2 * PAIRS].bitcast(BF16)
+        z_codes = mx_tiles("z_codes", U32, HALF, [(0, 0), (1, 0), (1, 1)])
+        z_scales = mx_tiles("z_scales", U8, HALF, pass_pairs)
 
-        def load_tab(a):
-            nc.sync.dma_start(tabw[a][:].bitcast(I32), tab_words[a].rearrange("p t i -> p (t i)").bitcast(I32))
+        bed_slices = bed.rearrange("(b p t) j -> b t p j", b=PASSES, t=PACK)
 
-        def load_raw(w, a, c0, width):
+        def load_table_words(a):
+            nc.sync.dma_start(table_words[a][:].bitcast(I32), tab_words[a].rearrange("p t i -> p (t i)").bitcast(I32))
+
+        def load_weight(w, a, c0, width):
             raw = raws.tile([P, PACK, width], F32, name=f"raw{width}")
-            nc.sync.dma_start(raw[:], w[a * PASS : (a + 1) * PASS, c0 : c0 + width].rearrange("(p i) c -> p i c", i=PACK))
+            rows = w[a * PASS : (a + 1) * PASS, c0 : c0 + width]
+            nc.sync.dma_start(raw[:], rows.rearrange("(p i) c -> p i c", i=PACK))
             return raw
 
-        def load_bed(u):
-            nc.sync.dma_start(beds[u][:], bed_rows[u // PACK, u % PACK])
+        def load_bed(u, j0=0, width=S):
+            nc.sync.dma_start(x[u][:, j0 : j0 + width], bed_slices[u // PACK, u % PACK][:, j0 : j0 + width])
 
-        def cast_w1(grouped, raw, r0, q0, nq):
+        def new_rounded():
+            return rounded.tile([P, PASS * PACK], BF16, name="rounded_w", align_bytes=64)
+
+        def round_w1(dst, raw, q0, half):
+            count = raw.shape[2] // PACK
             nc.scalar.copy(
-                grouped[:].rearrange("p (t q i) -> p q i t", t=PACK, i=PACK)[:, q0 : q0 + nq],
-                raw[:].rearrange("p i (q t) -> p q i t", t=PACK)[:, r0 : r0 + nq],
+                dst[:].rearrange("p (h t q i) -> p h q i t", h=2, t=2, i=PACK)[:, half, q0 : q0 + count],
+                raw[:].rearrange("p i (q h t) -> p h q i t", h=2, t=2)[:, half],
             )
 
-        def cast_w3(grouped, raw, c0, width):
-            nc.scalar.copy(
-                grouped[:].rearrange("p (c n i) -> p c i n", n=PACK, i=PACK)[:, c0 // PACK : (c0 + width) // PACK],
-                raw[:].rearrange("p i (c n) -> p c i n", n=PACK)[:, c0 // PACK : (c0 + width) // PACK],
+        def interleave(copy, dst, src):
+            copy(
+                dst.rearrange("p (c n i) -> p c i n", n=2, i=PACK),
+                src.rearrange("p i (c n) -> p c i n", n=2),
             )
-
-        def new_group():
-            return grps.tile([P, PASS * PACK], BF16, name="grouped", align_bytes=64)
 
         def quantize(codes, scales, src):
-            nc.vector.quantize_mx(out=codes.bitcast(FP8X4), scales=scales, in_=src)
+            nc.vector.quantize_mx(out=codes[:].bitcast(FP8X4), scales=scales[:], in_=src)
 
-        nc.vector.memset(tabs[:].bitcast(I32), 0)
-        nc.gpsimd.memset(w4s[:].rearrange("p b c -> p (b c)").bitcast(I32), 0)
-        nc.gpsimd.memset(warm[:], 0.0)
-        nc.scalar.activation(warm[:], warm[:], ACT.Silu)
+        def round_w1_head(halves):
+            dst = new_rounded()
+            for c in BOTH:
+                for half in BOTH:
+                    round_w1(dst, halves[c][:], c * PIECE // PACK, half)
+            return dst
+
+        nc.gpsimd.memset(table_scales[:, 0 : T // 2].bitcast(I32), 0)
+        nc.vector.memset(table_scales[:, T // 2 : T].bitcast(I32), 0)
+        nc.gpsimd.memset(w4_scales_sb[:].rearrange("p b c -> p (b c)").bitcast(I32), 0)
+
         nc.sync.dma_start(offs_sb[:], offs)
-        raw00 = [load_raw(w1, 0, c * 256, 256) for c in range(2)]
-        for a in range(2):
+        load_table_words(0)
+        head_raw = {0: [load_weight(w1, 0, 0, PIECE)]}
+        for a in BOTH:
             rows = tab_scales[a].rearrange("(g e) t -> e g t", e=2)
-            for e in range(2):
-                nc.sync.dma_start(tabs[8 * a + e : P : 16, :].bitcast(I32), rows[e].bitcast(I32))
-        load_tab(0)
-        raw10 = [load_raw(w1, 1, c * 256, 256) for c in range(2)]
-        load_tab(1)
-        load_bed(0)
+            for e in BOTH:
+                nc.sync.dma_start(table_scales[PLANE_STEP * a + e : P : GROUP, :].bitcast(I32), rows[e].bitcast(I32))
+        head_raw[0].append(load_weight(w1, 0, PIECE, PIECE))
+        head_raw[1] = [load_weight(w1, 1, c * PIECE, PIECE) for c in BOTH]
+        load_table_words(1)
+        for c in BOTH:
+            load_bed(0, c * BANK, BANK)
         nc.sync.dma_start(pos2_sb[:], pos2)
         nc.sync.dma_start(pos1_sb[:], pos1)
-        nc.sync.dma_start(gain_sb[:], gain.rearrange("(b p t) -> p b t", b=2, t=PACK))
+        nc.sync.dma_start(gain_sb[:], gain.rearrange("(b p t) -> p b t", b=PASSES, t=PACK))
 
-        nc.vector.tensor_copy(picked_s[:], tabs[:].indirect(offs_sb[:]))
-        nc.vector.tensor_copy(v_scales[:].bitcast(I32), picked_s[:].bitcast(I32))
-        nc.vector.tensor_copy(v_words[0][:], tabw[0][:].indirect(offs_sb[:]))
-        g00 = new_group()
-        for c in range(2):
-            cast_w1(g00, raw00[c], 0, c * 64, 64)
-        for e in range(2):
+        nc.vector.tensor_copy(v_words[0][:], table_words[0][:].indirect(offs_sb[:]))
+        nc.vector.tensor_copy(picked_scales[:], table_scales[:].indirect(offs_sb[:]))
+        nc.vector.tensor_copy(v_scales[:].bitcast(I32), picked_scales[:].bitcast(I32))
+        w1_head = round_w1_head(head_raw[0])
+        for e in BOTH:
             nc.sync.dma_start(
-                v_scales[2 + e : P - 16 : 8, :].bitcast(I32),
-                picked_s[16 + e : P : 8, :].bitcast(I32),
+                v_scales[2 + e : P - GROUP : PLANE_STEP, :].bitcast(I32),
+                picked_scales[GROUP + e : P : PLANE_STEP, :].bitcast(I32),
             )
-        quantize(w1c[0, 0][:], w1s[0, 0][:], g00[:])
-        g10 = new_group()
-        for c in range(2):
-            cast_w1(g10, raw10[c], 0, c * 64, 64)
-        quantize(w1c[1, 0][:], w1s[1, 0][:], g10[:])
-        for c in range(2):
-            nc.vector.tensor_copy(
-                v_words[1][:, c * BANK : (c + 1) * BANK], tabw[1][:].indirect(offs_sb[:, c * 32 : (c + 1) * 32])
-            )
-        nc.gpsimd.tensor_scalar(ngain[:], gain_sb[:], -1.0, 0.0, ALU.mult, ALU.add)
+        quantize(w1_codes[0, 0], w1_scales[0, 0], w1_head[:])
+        w1_head = round_w1_head(head_raw[1])
+        quantize(w1_codes[1, 0], w1_scales[1, 0], w1_head[:])
+        for c in BOTH:
+            entries = offs_sb[:, c * BANK // GROUP : (c + 1) * BANK // GROUP]
+            nc.vector.tensor_copy(v_words[1][:, c * BANK : (c + 1) * BANK], table_words[1][:].indirect(entries))
+        nc.gpsimd.tensor_scalar(minus_gain[:], gain_sb[:], -1.0, 0.0, ALU.mult, ALU.add)
 
-        raw_next = [load_raw(w1, 0, PASS, PASS)]
-        for u in (1, 2):
+        later_raw = []
+        for u in range(1, SLICES):
             load_bed(u)
-        raw_next.append(load_raw(w1, 1, PASS, PASS))
-        load_bed(3)
-        for b in range(2):
-            raw_next.append(load_raw(w3, b, 0, N))
-            load_bed(4 + b)
-        for u in (6, 7):
-            load_bed(u)
-        nc.sync.dma_start(w4w[:].bitcast(I32), w4_words.rearrange("b p c -> p b c").bitcast(I32))
+            if u in (1, 2):
+                later_raw.append(load_weight(w1, u - 1, PASS, PASS))
+            if u in (3, 4):
+                later_raw.append(load_weight(w3, u - 3, 0, N))
+        nc.sync.dma_start(w4_sb[:].bitcast(I32), w4_words.rearrange("b p c -> p b c").bitcast(I32))
         for d in range(4):
             nc.sync.dma_start(
-                w4s[32 * d : 32 * d + 4].bitcast(I32),
+                w4_scales_sb[32 * d : 32 * d + 4].bitcast(I32),
                 w4_scales[:, 4 * d : 4 * d + 4, :].rearrange("b q c -> q b c").bitcast(I32),
             )
 
         h = {}
         factor = {}
+        scores = {}
 
         def first_stage(u):
             b, t = divmod(u, PACK)
-            cols = slice(t * P, (t + 1) * P)
-            for c in range(2):
+            rows = slice(t * P, (t + 1) * P)
+            for c in BOTH:
                 js = slice(c * BANK, (c + 1) * BANK)
                 acc = psum.tile([P, BANK], F32, name="acc")
-                for a in range(2):
+                for a in BOTH:
                     nc.tensor.matmul_mx(
                         out=acc[:],
-                        lhsT=w1c[a, b][:, cols].bitcast(FP8X4),
-                        lhsT_scale=w1s[a, b][:, cols],
+                        lhsT=w1_codes[a, b][:, rows].bitcast(FP8X4),
+                        lhsT_scale=w1_scales[a, b][:, rows],
                         rhs=v_words[a][:, js].bitcast(FP8X4),
-                        rhs_scale=v_scales[8 * a : P, js],
+                        rhs_scale=v_scales[PLANE_STEP * a : P, js],
                         start=(a == 0),
                         stop=(a == 1),
                     )
-                nc.vector.tensor_tensor(beds[u][:, js], acc[:], beds[u][:, js], ALU.add)
+                nc.vector.tensor_tensor(x[u][:, js], acc[:], x[u][:, js], ALU.add)
             h[u] = hs.tile([P, S], F32, name="h")
-            nc.scalar.activation(h[u][:], beds[u][:], ACT.Silu)
+            nc.scalar.activation(h[u][:], x[u][:], ACT.Silu)
 
         def second_course(u):
             b, t = divmod(u, PACK)
-            if u == 7:
-                second = last[:, 0:PAIRS]
-            else:
-                second = seconds.tile([P, PAIRS], F32, name="second")[:]
+            second = tail[:, 0:PAIRS] if u == SLICES - 1 else seconds.tile([P, PAIRS], F32, name="second")[:]
             nc.vector.tensor_copy(second, h[u][:].indirect(pos2_sb[:]))
             factor[u] = work.tile([P, PAIRS], F32, name="factor", align_bytes=64)
             nc.scalar.activation(
-                factor[u][:], second, ACT.Identity, bias=ngain[:, b, t : t + 1], scale=gain_sb[:, b, t : t + 1]
+                factor[u][:], second, ACT.Identity, bias=minus_gain[:, b, t : t + 1], scale=gain_sb[:, b, t : t + 1]
             )
 
-        def first_course(u, m0, width):
-            b, t = divmod(u, PACK)
-            nc.vector.tensor_tensor(
-                zf[0][:, t, :] if b == 0 else zf[1, m0 // HALF][:, t, :],
-                h[u][:].indirect(pos1_sb[:, m0 // 16 : (m0 + width) // 16]),
-                factor[u][:, m0 : m0 + width],
-                ALU.mult,
-            )
+        def first_course(u, dst, m0):
+            width = dst.shape[1]
+            first = h[u][:].indirect(pos1_sb[:, m0 // GROUP : (m0 + width) // GROUP])
+            nc.vector.tensor_tensor(dst, first, factor[u][:, m0 : m0 + width], ALU.mult)
 
-        def round_z(b, c, copy):
-            src = zf[0][:, :, c * HALF : (c + 1) * HALF] if b == 0 else zf[1, c]
-            copy(
-                zb[b, c].rearrange("p (m n t) -> p m t n", n=PACK, t=PACK),
-                src.rearrange("p t (m n) -> p m t n", n=PACK),
-            )
+        def later_weight(n):
+            dst = new_rounded()
+            for c in BOTH:
+                if n < PASSES:
+                    round_w1(dst, later_raw[n][:], 0, c)
+                else:
+                    cols = slice(c * PIECE, (c + 1) * PIECE)
+                    interleave(nc.scalar.copy, dst[:, PACK * cols.start : PACK * cols.stop], later_raw[n][:, :, cols])
+            if n < PASSES:
+                quantize(w1_codes[n, 1], w1_scales[n, 1], dst[:])
+            else:
+                quantize(w3_codes[n - PASSES], w3_scales[n - PASSES], dst[:])
 
         def quantize_z(b, c):
-            quantize(zc[b, c][:], zs[b, c][:], zb[b, c])
-
-        scores = {}
+            quantize(z_codes[b, c], z_scales[b, c], z_bf16[b, c])
 
         def second_stage(b, c):
-            for pair in range(2):
+            for g in BOTH:
                 if b == 0:
-                    scores[3, pair, c] = psum.tile([P, BANK], F32, name="acc")
-                    scores[4, pair, c] = psum.tile([P, BANK], F32, name="acc")
-                for k in range(2):
-                    n = 2 * pair + k
-                    cols = slice(n * P, (n + 1) * P)
+                    scores["w3", g, c] = psum.tile([P, BANK], F32, name="acc")
+                    scores["w4", g, c] = psum.tile([P, BANK], F32, name="acc")
+                for k in BOTH:
+                    faults = slice((2 * g + k) * P, (2 * g + k + 1) * P)
                     nc.tensor.matmul_mx(
-                        out=scores[3, pair, c][:, k * HALF : (k + 1) * HALF],
-                        lhsT=w3c[b][:, cols].bitcast(FP8X4),
-                        lhsT_scale=w3s[b][:, cols],
-                        rhs=zc[b, c][:].bitcast(FP8X4),
-                        rhs_scale=zs[b, c][:],
+                        out=scores["w3", g, c][:, k * HALF : (k + 1) * HALF],
+                        lhsT=w3_codes[b][:, faults].bitcast(FP8X4),
+                        lhsT_scale=w3_scales[b][:, faults],
+                        rhs=z_codes[b, c][:].bitcast(FP8X4),
+                        rhs_scale=z_scales[b, c][:],
                         start=(b == 0 and k == 0),
                         stop=(b == 1 and k == 1),
                     )
-                for k in range(2):
-                    n = 2 * pair + k
-                    cols = slice(n * P, (n + 1) * P)
-                    for s in range(2):
+                for k in BOTH:
+                    faults = slice((2 * g + k) * P, (2 * g + k + 1) * P)
+                    for s in BOTH:
                         ms = slice(s * P, (s + 1) * P)
                         nc.tensor.matmul_mx(
-                            out=scores[4, pair, c][:, k * HALF + s * P : k * HALF + (s + 1) * P],
-                            lhsT=w4w[:, b, 2 * n * P : 2 * (n + 1) * P].bitcast(FP4X4),
-                            lhsT_scale=w4s[:, b, cols],
-                            rhs=zc[b, c][:, ms].bitcast(FP8X4),
-                            rhs_scale=zs[b, c][:, ms],
+                            out=scores["w4", g, c][:, k * HALF + s * P : k * HALF + (s + 1) * P],
+                            lhsT=w4_sb[:, b, 2 * faults.start : 2 * faults.stop].bitcast(FP4X4),
+                            lhsT_scale=w4_scales_sb[:, b, faults],
+                            rhs=z_codes[b, c][:, ms].bitcast(FP8X4),
+                            rhs_scale=z_scales[b, c][:, ms],
                             start=(b == 0 and k == 0 and s == 0),
                             stop=(b == 1 and k == 1 and s == 1),
                         )
 
         def finish(c):
-            for pair in range(2):
+            for g in BOTH:
                 y3 = work.tile([P, BANK], F32, name="y3")
-                nc.scalar.copy(y3[:], scores[3, pair, c][:])
-                res = work.tile([P, BANK], F32, name="res")
-                nc.vector.tensor_tensor(res[:], scores[4, pair, c][:], y3[:], ALU.min)
+                nc.scalar.copy(y3[:], scores["w3", g, c][:])
+                smaller = work.tile([P, BANK], F32, name="smaller")
+                nc.vector.tensor_tensor(smaller[:], scores["w4", g, c][:], y3[:], ALU.min)
                 nc.sync.dma_start(
-                    out[2 * pair * P : 2 * (pair + 1) * P, c * HALF : (c + 1) * HALF].rearrange("(k p) m -> p k m", k=2),
-                    res[:].rearrange("p (k m) -> p k m", k=2),
+                    out[2 * g * P : 2 * (g + 1) * P, c * HALF : (c + 1) * HALF].rearrange("(k p) m -> p k m", k=2),
+                    smaller[:].rearrange("p (k m) -> p k m", k=2),
                 )
 
-        groups = {}
-
-        def later_weight(piece):
-            idx, c = divmod(piece, 2)
-            if c == 0:
-                groups[idx] = new_group()
-            if idx < 2:
-                cast_w1(groups[idx], raw_next[idx], c * 64, c * 64, 64)
-                codes, scales = w1c[idx, 1], w1s[idx, 1]
-            else:
-                cast_w3(groups[idx], raw_next[idx], c * 256, 256)
-                codes, scales = w3c[idx - 2], w3s[idx - 2]
-            if c == 1:
-                quantize(codes[:], scales[:], groups[idx][:])
-
         first_stage(0)
-        for u in range(8):
-            if u + 1 < 8:
+        for u in range(SLICES):
+            if u + 1 < SLICES:
                 first_stage(u + 1)
             second_course(u)
-            if u < 4:
-                later_weight(2 * u)
-                later_weight(2 * u + 1)
-            if 1 <= u <= 4:
-                first_course(u - 1, 0, PAIRS)
-            elif u > 4:
-                first_course(u - 1, 0, HALF)
-            if u in (4, 5):
-                round_z(0, u - 4, nc.scalar.copy)
-            if u == 5:
+            if u < len(later_raw):
+                later_weight(u)
+            if 1 <= u <= PACK:
+                first_course(u - 1, z_first[:, u - 1, :], 0)
+            elif u > PACK:
+                first_course(u - 1, z_f32[1, 0][:, u - 1 - PACK, :], 0)
+            if u in (PACK, PACK + 1):
+                interleave(nc.scalar.copy, z_bf16[0, u - PACK], z_f32[0, u - PACK])
+            if u == PACK + 1:
                 quantize_z(0, 0)
-        first_course(7, 0, HALF)
+        first_course(SLICES - 1, z_f32[1, 0][:, PACK - 1, :], 0)
         second_stage(0, 0)
-        round_z(1, 0, nc.scalar.copy)
-        first_course(4, HALF, HALF)
-        first_course(5, HALF, HALF)
+        interleave(nc.scalar.copy, z_bf16[1, 0], z_f32[1, 0])
+        for t in (0, 1):
+            first_course(PACK + t, z_f32[1, 1][:, t, :], HALF)
         quantize_z(1, 0)
         second_stage(1, 0)
-        zc[0, 1] = work.tile([P, HALF], U32, name="factor", align_bytes=64)
+        z_codes[0, 1] = work.tile([P, HALF], U32, name="factor", align_bytes=64)
         quantize_z(0, 1)
         second_stage(0, 1)
-        first_course(6, HALF, HALF)
-        first_course(7, HALF, HALF)
-        round_z(1, 1, nc.vector.tensor_copy)
+        for t in (2, 3):
+            first_course(PACK + t, z_f32[1, 1][:, t, :], HALF)
+        interleave(nc.vector.tensor_copy, z_bf16[1, 1], z_f32[1, 1])
         quantize_z(1, 1)
         second_stage(1, 1)
         finish(0)

from contextlib import ExitStack

import concourse.mybir as mybir

K, T, S, H, PAIRS, N = 1024, 2048, 1024, 1024, 512, 512
FLOPS = 2 * K * H * S + 2 * 2 * H * N * PAIRS

F32 = mybir.dt.float32
BF16 = mybir.dt.bfloat16
I32 = mybir.dt.int32
U32 = mybir.dt.uint32
U16 = mybir.dt.uint16
U8 = mybir.dt.uint8
FP8X4 = mybir.dt.float8_e4m3fn_x4
FP4X4 = mybir.dt.float4_e2m1fn_x4
ALU = mybir.AluOpType
ACT = mybir.ActivationFunctionType

P = 128
GROUP = 16
PACK = 4
PASS = P * PACK
PASSES = 2
SLICES = PASSES * PACK
BANK = 512
HALF = PAIRS // 2
PIECE = PASS // 2
PLANE_STEP = 8
BOTH = range(2)


def tile_list_feeder_fault_scores_kernel(
    tc, tab_words, tab_scales, offs, pos1, pos2, w1, bed, gain, w3, w4_words, w4_scales, out
):
    nc = tc.nc
    with ExitStack() as ctx:
        keep = ctx.enter_context(tc.tile_pool(name="keep", bufs=1))
        raws = ctx.enter_context(tc.tile_pool(name="raws", bufs=4))
        rounded = ctx.enter_context(tc.tile_pool(name="rounded", bufs=3))
        hs = ctx.enter_context(tc.tile_pool(name="hs", bufs=PACK + 1))
        work = ctx.enter_context(tc.tile_pool(name="work", bufs=PACK))
        seconds = ctx.enter_context(tc.tile_pool(name="seconds", bufs=2))
        psum = ctx.enter_context(tc.psum_pool(name="psum", bufs=8))

        def mx_tiles(name, dtype, width, keys):
            return {key: keep.tile([P, width], dtype, name=f"{name}{n}", align_bytes=64) for n, key in enumerate(keys)}

        pass_pairs = [(a, b) for a in BOTH for b in BOTH]
        offs_sb = keep.tile([P, S // GROUP], U16, name="offs_sb")
        pos1_sb = keep.tile([P, PAIRS // GROUP], U16, name="pos1_sb")
        pos2_sb = keep.tile([P, PAIRS // GROUP], U16, name="pos2_sb")
        gain_sb = keep.tile([P, PASSES, PACK], F32, name="gain_sb")
        minus_gain = keep.tile([P, PASSES, PACK], F32, name="minus_gain")
        table_words = mx_tiles("table_words", U32, T, BOTH)
        table_scales = keep.tile([P, T], U8, name="table_scales", align_bytes=64)
        picked_scales = keep.tile([P, S], U8, name="picked_scales", align_bytes=64)
        v_scales = keep.tile([P, S], U8, name="v_scales", align_bytes=64)
        v_words = mx_tiles("v_words", U32, S, BOTH)
        w1_codes = mx_tiles("w1_codes", U32, PASS, pass_pairs)
        w1_scales = mx_tiles("w1_scales", U8, PASS, pass_pairs)
        w3_codes = mx_tiles("w3_codes", U32, N, BOTH)
        w3_scales = mx_tiles("w3_scales", U8, N, BOTH)
        w4_sb = keep.tile([P, PASSES, 2 * N], U8, name="w4_sb", align_bytes=64)
        w4_scales_sb = keep.tile([P, PASSES, N], U8, name="w4_scales_sb", align_bytes=64)
        x = [keep.tile([P, S], F32, name=f"x{u}") for u in range(SLICES)]

        z_first = keep.tile([P, PACK, PAIRS], F32, name="z_first")
        z_last_low = keep.tile([P, PACK, HALF], F32, name="z_last_low")
        tail = keep.tile([P, PACK * HALF], F32, name="tail", align_bytes=64)
        z_f32 = {(0, c): z_first[:, :, c * HALF : (c + 1) * HALF] for c in BOTH}
        z_f32[1, 0] = z_last_low[:]
        z_f32[1, 1] = tail[:].rearrange("p (t m) -> p t m", t=PACK)
        z_bf16 = {key: tile[:] for key, tile in mx_tiles("z_bf16", BF16, PACK * HALF, [(0, 0), (0, 1), (1, 1)]).items()}
        z_bf16[1, 0] = tail[:, PAIRS : 2 * PAIRS].bitcast(BF16)
        z_codes = mx_tiles("z_codes", U32, HALF, [(0, 0), (1, 0), (1, 1)])
        z_scales = mx_tiles("z_scales", U8, HALF, pass_pairs)

        bed_slices = bed.rearrange("(b p t) j -> b t p j", b=PASSES, t=PACK)

        def load_table_words(a):
            nc.sync.dma_start(table_words[a][:].bitcast(I32), tab_words[a].rearrange("p t i -> p (t i)").bitcast(I32))

        def load_weight(w, a, c0, width):
            raw = raws.tile([P, PACK, width], F32, name=f"raw{width}")
            rows = w[a * PASS : (a + 1) * PASS, c0 : c0 + width]
            nc.sync.dma_start(raw[:], rows.rearrange("(p i) c -> p i c", i=PACK))
            return raw

        def load_bed(u, j0=0, width=S):
            nc.sync.dma_start(x[u][:, j0 : j0 + width], bed_slices[u // PACK, u % PACK][:, j0 : j0 + width])

        def new_rounded():
            return rounded.tile([P, PASS * PACK], BF16, name="rounded_w", align_bytes=64)

        def round_w1(dst, raw, q0, half):
            count = raw.shape[2] // PACK
            nc.scalar.copy(
                dst[:].rearrange("p (h t q i) -> p h q i t", h=2, t=2, i=PACK)[:, half, q0 : q0 + count],
                raw[:].rearrange("p i (q h t) -> p h q i t", h=2, t=2)[:, half],
            )

        def interleave(copy, dst, src):
            copy(
                dst.rearrange("p (c n i) -> p c i n", n=2, i=PACK),
                src.rearrange("p i (c n) -> p c i n", n=2),
            )

        def quantize(codes, scales, src):
            nc.vector.quantize_mx(out=codes[:].bitcast(FP8X4), scales=scales[:], in_=src)

        def round_w1_head(halves):
            dst = new_rounded()
            for c in BOTH:
                for half in BOTH:
                    round_w1(dst, halves[c][:], c * PIECE // PACK, half)
            return dst

        nc.gpsimd.memset(table_scales[:, 0 : T // 2].bitcast(I32), 0)
        nc.vector.memset(table_scales[:, T // 2 : T].bitcast(I32), 0)
        nc.gpsimd.memset(w4_scales_sb[:].rearrange("p b c -> p (b c)").bitcast(I32), 0)

        nc.sync.dma_start(offs_sb[:], offs)
        load_table_words(0)
        head_raw = {0: [load_weight(w1, 0, 0, PIECE)]}
        for a in BOTH:
            rows = tab_scales[a].rearrange("(g e) t -> e g t", e=2)
            for e in BOTH:
                nc.sync.dma_start(table_scales[PLANE_STEP * a + e : P : GROUP, :].bitcast(I32), rows[e].bitcast(I32))
        head_raw[0].append(load_weight(w1, 0, PIECE, PIECE))
        head_raw[1] = [load_weight(w1, 1, c * PIECE, PIECE) for c in BOTH]
        load_table_words(1)
        for c in BOTH:
            load_bed(0, c * BANK, BANK)
        nc.sync.dma_start(pos2_sb[:], pos2)
        nc.sync.dma_start(pos1_sb[:], pos1)
        nc.sync.dma_start(gain_sb[:], gain.rearrange("(b p t) -> p b t", b=PASSES, t=PACK))

        nc.vector.tensor_copy(v_words[0][:], table_words[0][:].indirect(offs_sb[:]))
        nc.vector.tensor_copy(picked_scales[:], table_scales[:].indirect(offs_sb[:]))
        nc.vector.tensor_copy(v_scales[:].bitcast(I32), picked_scales[:].bitcast(I32))
        w1_head = round_w1_head(head_raw[0])
        for e in BOTH:
            nc.sync.dma_start(
                v_scales[2 + e : P - GROUP : PLANE_STEP, :].bitcast(I32),
                picked_scales[GROUP + e : P : PLANE_STEP, :].bitcast(I32),
            )
        quantize(w1_codes[0, 0], w1_scales[0, 0], w1_head[:])
        w1_head = round_w1_head(head_raw[1])
        quantize(w1_codes[1, 0], w1_scales[1, 0], w1_head[:])
        for c in BOTH:
            entries = offs_sb[:, c * BANK // GROUP : (c + 1) * BANK // GROUP]
            nc.vector.tensor_copy(v_words[1][:, c * BANK : (c + 1) * BANK], table_words[1][:].indirect(entries))
        nc.gpsimd.tensor_scalar(minus_gain[:], gain_sb[:], -1.0, 0.0, ALU.mult, ALU.add)

        later_raw = []
        for u in range(1, SLICES):
            load_bed(u)
            if u in (1, 2):
                later_raw.append(load_weight(w1, u - 1, PASS, PASS))
            if u in (3, 4):
                later_raw.append(load_weight(w3, u - 3, 0, N))
        nc.sync.dma_start(w4_sb[:].bitcast(I32), w4_words.rearrange("b p c -> p b c").bitcast(I32))
        for d in range(4):
            nc.sync.dma_start(
                w4_scales_sb[32 * d : 32 * d + 4].bitcast(I32),
                w4_scales[:, 4 * d : 4 * d + 4, :].rearrange("b q c -> q b c").bitcast(I32),
            )

        h = {}
        factor = {}
        scores = {}

        def first_stage(u):
            b, t = divmod(u, PACK)
            rows = slice(t * P, (t + 1) * P)
            for c in BOTH:
                js = slice(c * BANK, (c + 1) * BANK)
                acc = psum.tile([P, BANK], F32, name="acc")
                for a in BOTH:
                    nc.tensor.matmul_mx(
                        out=acc[:],
                        lhsT=w1_codes[a, b][:, rows].bitcast(FP8X4),
                        lhsT_scale=w1_scales[a, b][:, rows],
                        rhs=v_words[a][:, js].bitcast(FP8X4),
                        rhs_scale=v_scales[PLANE_STEP * a : P, js],
                        start=(a == 0),
                        stop=(a == 1),
                    )
                nc.vector.tensor_tensor(x[u][:, js], acc[:], x[u][:, js], ALU.add)
            h[u] = hs.tile([P, S], F32, name="h")
            nc.scalar.activation(h[u][:], x[u][:], ACT.Silu)

        def second_course(u):
            b, t = divmod(u, PACK)
            second = tail[:, 0:PAIRS] if u == SLICES - 1 else seconds.tile([P, PAIRS], F32, name="second")[:]
            nc.vector.tensor_copy(second, h[u][:].indirect(pos2_sb[:]))
            factor[u] = work.tile([P, PAIRS], F32, name="factor", align_bytes=64)
            nc.scalar.activation(
                factor[u][:], second, ACT.Identity, bias=minus_gain[:, b, t : t + 1], scale=gain_sb[:, b, t : t + 1]
            )

        def first_course(u, dst, m0):
            width = dst.shape[1]
            first = h[u][:].indirect(pos1_sb[:, m0 // GROUP : (m0 + width) // GROUP])
            nc.vector.tensor_tensor(dst, first, factor[u][:, m0 : m0 + width], ALU.mult)

        def later_weight(n):
            dst = new_rounded()
            for c in BOTH:
                if n < PASSES:
                    round_w1(dst, later_raw[n][:], 0, c)
                else:
                    cols = slice(c * PIECE, (c + 1) * PIECE)
                    interleave(nc.scalar.copy, dst[:, PACK * cols.start : PACK * cols.stop], later_raw[n][:, :, cols])
            if n < PASSES:
                quantize(w1_codes[n, 1], w1_scales[n, 1], dst[:])
            else:
                quantize(w3_codes[n - PASSES], w3_scales[n - PASSES], dst[:])

        def quantize_z(b, c):
            quantize(z_codes[b, c], z_scales[b, c], z_bf16[b, c])

        def second_stage(b, c):
            for g in BOTH:
                if b == 0:
                    scores["w3", g, c] = psum.tile([P, BANK], F32, name="acc")
                    scores["w4", g, c] = psum.tile([P, BANK], F32, name="acc")
                for k in BOTH:
                    faults = slice((2 * g + k) * P, (2 * g + k + 1) * P)
                    nc.tensor.matmul_mx(
                        out=scores["w3", g, c][:, k * HALF : (k + 1) * HALF],
                        lhsT=w3_codes[b][:, faults].bitcast(FP8X4),
                        lhsT_scale=w3_scales[b][:, faults],
                        rhs=z_codes[b, c][:].bitcast(FP8X4),
                        rhs_scale=z_scales[b, c][:],
                        start=(b == 0 and k == 0),
                        stop=(b == 1 and k == 1),
                    )
                for k in BOTH:
                    faults = slice((2 * g + k) * P, (2 * g + k + 1) * P)
                    for s in BOTH:
                        ms = slice(s * P, (s + 1) * P)
                        nc.tensor.matmul_mx(
                            out=scores["w4", g, c][:, k * HALF + s * P : k * HALF + (s + 1) * P],
                            lhsT=w4_sb[:, b, 2 * faults.start : 2 * faults.stop].bitcast(FP4X4),
                            lhsT_scale=w4_scales_sb[:, b, faults],
                            rhs=z_codes[b, c][:, ms].bitcast(FP8X4),
                            rhs_scale=z_scales[b, c][:, ms],
                            start=(b == 0 and k == 0 and s == 0),
                            stop=(b == 1 and k == 1 and s == 1),
                        )

        def finish(c):
            for g in BOTH:
                y3 = work.tile([P, BANK], F32, name="y3")
                nc.scalar.copy(y3[:], scores["w3", g, c][:])
                smaller = work.tile([P, BANK], F32, name="smaller")
                nc.vector.tensor_tensor(smaller[:], scores["w4", g, c][:], y3[:], ALU.min)
                nc.sync.dma_start(
                    out[2 * g * P : 2 * (g + 1) * P, c * HALF : (c + 1) * HALF].rearrange("(k p) m -> p k m", k=2),
                    smaller[:].rearrange("p (k m) -> p k m", k=2),
                )

        first_stage(0)
        for u in range(SLICES):
            if u + 1 < SLICES:
                first_stage(u + 1)
            second_course(u)
            if u < len(later_raw):
                later_weight(u)
            if 1 <= u <= PACK:
                first_course(u - 1, z_first[:, u - 1, :], 0)
            elif u > PACK:
                first_course(u - 1, z_f32[1, 0][:, u - 1 - PACK, :], 0)
            if u in (PACK, PACK + 1):
                interleave(nc.scalar.copy, z_bf16[0, u - PACK], z_f32[0, u - PACK])
            if u == PACK + 1:
                quantize_z(0, 0)
        first_course(SLICES - 1, z_f32[1, 0][:, PACK - 1, :], 0)
        second_stage(0, 0)
        interleave(nc.scalar.copy, z_bf16[1, 0], z_f32[1, 0])
        for t in (0, 1):
            first_course(PACK + t, z_f32[1, 1][:, t, :], HALF)
        quantize_z(1, 0)
        second_stage(1, 0)
        z_codes[0, 1] = work.tile([P, HALF], U32, name="factor", align_bytes=64)
        quantize_z(0, 1)
        second_stage(0, 1)
        for t in (2, 3):
            first_course(PACK + t, z_f32[1, 1][:, t, :], HALF)
        interleave(nc.vector.tensor_copy, z_bf16[1, 1], z_f32[1, 1])
        quantize_z(1, 1)
        second_stage(1, 1)
        finish(0)
        finish(1)
